import numpy as np, ml_dtypes
CORES = [13,21,141,149]
N = 4
BF = ml_dtypes.bfloat16
def gentries(a):
    return np.ascontiguousarray(a.reshape(8, 16, -1).transpose(0, 2, 1)).reshape(8, -1)
def gtable(e):
    e = np.asarray(e); return np.ascontiguousarray(e.reshape(8, -1, 16).transpose(0, 2, 1)).reshape(128, -1).astype(np.int32)
C, CAP, P, H = 896, 320, 4096, 3
def walk(cells, first, pads):
    x = cells.astype(np.float32).astype(np.int32).reshape(N, 8, 16, C); p = pads.astype(np.float32).astype(np.int32).reshape(N, 8, 16, P)
    keys = [gentries(a) for a in first]; most = 0; sent = {}
    now = {(r, g): (x[r, g], keys[r][g]) for r in range(N) for g in range(8)}
    for h in range(H):
        sent = {}
        for r in range(N):
            for g in range(8):
                v, key = now[r, g]; v = (v - p[r, g][:, key]) & 255
                to = v[0] & (N - 1); key = v[1] + 256 * (v[2] & (P // 256 - 1))
                for q in range(N):
                    m = to == q; sent[r, q, g] = (v[:, m], key[m]); most = max(most, int(np.count_nonzero(m)))
        now = {(q, g): (np.concatenate([sent[r, q, g][0] for r in range(N)], axis=1), np.concatenate([sent[r, q, g][1] for r in range(N)])) for q in range(N) for g in range(8)}
    return sent, most
def parts(rng, n, w, t=-1):
    w = np.array(w, np.float64); k = 0
    if t >= 0:
        w[t] = 0; k = min(n, CAP)
    a = np.add.accumulate(w); i = np.searchsorted(a, rng.random(n - k) * a[-1], side="right")
    c = np.minimum(np.bincount(np.minimum(i, N - 1), minlength=N), CAP)
    if t >= 0: c[t] = k
    o = rng.permutation(N); o = o[np.argsort(w[o] == 0, kind="stable")]
    for r in o: c[r] += min(n - int(np.sum(c)), CAP - int(c[r]))
    return c
def routes(rng, count, runs=False):
    to = np.zeros((8, N, C, H), np.int64)
    for g in range(8):
        at = np.repeat(np.arange(N), C); t = to[g].reshape(N * C, H)
        for h in range(H):
            new = at.copy()
            for q in range(N):
                i = np.nonzero(at == q)[0]; d = np.repeat(np.arange(N), count(h, g, q, len(i)))
                new[i] = d if runs and g % 2 == 0 else rng.permutation(d)
            t[:, h] = new; at = new
    return to
def dress(to, first, p, body, u):
    x = body.copy()
    for g in range(8):
        for r in range(N):
            key = np.arange(P); at = np.full(P, r); v = np.stack([at, key & 255, key >> 8]); code = np.zeros(P, np.int64)
            for h in range(1, H):
                v = (v - np.stack([p[at, g, s, key] for s in range(3)])) & 255
                at = v[0] & (N - 1); key = v[1] + 256 * (v[2] & (P // 256 - 1)); code = code * N + at
            order = np.argsort(code, kind="stable"); a = np.searchsorted(code[order], np.arange(N ** (H - 1))); b = np.searchsorted(code[order], np.arange(N ** (H - 1)), side="right")
            q, i = np.nonzero(to[g, :, :, 0] == r); c = np.zeros(len(q), np.int64)
            for h in range(1, H): c = c * N + to[g, q, i, h]
            k = order[a[c] + np.floor(u[q, g, i] * (b - a)[c]).astype(np.int64)]
            x[q, g, 0, i] = x[q, g, 0, i] // N * N + r
            x[q, g, 1, i] = k & 255
            x[q, g, 2, i] = x[q, g, 2, i] // (P // 256) * (P // 256) + (k >> 8)
    x = (x + np.take_along_axis(p, first[:, :, None, :], axis=3)) & 255
    return {"cells": x.reshape(N, 128, C).astype(np.float32).astype(BF), "first": np.stack([gtable(e) for e in first]), "pads": p.reshape(N, 128, P).astype(np.float32).astype(BF)}
def setup_inputs(rng):
    w = 1 + rng.random((H, 8, N, N)); to = routes(rng, lambda h, g, q, n: parts(rng, n, w[h, g, q]))
    return dress(to, rng.integers(0, P, (N, 8, C)), rng.integers(0, 256, (N, 8, 16, P)), rng.integers(0, 256, (N, 8, 16, C)), rng.random((N, 8, C)))
def setup_inputs_ends(rng):
    w = 1 + rng.random((H, 8, N, N)); to = routes(rng, lambda h, g, q, n: parts(rng, n, w[h, g, q]))
    p = rng.integers(0, 256, (N, 8, 16, P)); p[0, :, :, 0] = 0
    full = rng.integers(0, 2, (N, 8, C)); body = rng.integers(0, 256, (N, 8, 16, C)) * full[:, :, None, :]
    u = rng.integers(0, 2, (N, 8, C)) * (1 - 2.0 ** -20)
    assert ((to == 0).all(axis=3).transpose(1, 0, 2) & (full == 0) & (u == 0)).any()
    return dress(to, rng.integers(0, 2, (N, 8, C)) * (P - 1), p, body, u)
def setup_inputs_full(rng):
    t = rng.integers(0, N, (H, 8)); to = routes(rng, lambda h, g, q, n: parts(rng, n, np.ones(N), int(t[h, g])), True)
    return dress(to, rng.integers(0, P, (N, 8, C)), rng.integers(0, 256, (N, 8, 16, P)), rng.integers(0, 256, (N, 8, 16, C)), rng.random((N, 8, C)))
def setup_inputs_bare(rng):
    s = rng.integers(0, N, H)
    def count(h, g, q, n):
        w = np.ones(N); none = (g % 2 == 0 and h == 0) or (g % 2 == 1 and h == H - 1)
        w[(g // 2 + s[h]) % N if none else (q + g + s[h]) % N] = 0
        return parts(rng, n, w)
    to = routes(rng, count)
    return dress(to, rng.integers(0, P, (N, 8, C)), rng.integers(0, 256, (N, 8, 16, P)), rng.integers(0, 256, (N, 8, 16, C)), rng.random((N, 8, C)))
def setup_inputs_spread(rng):
    w = np.exp2(rng.integers(-4, 5, (H, 8, N, N))); to = routes(rng, lambda h, g, q, n: parts(rng, n, w[h, g, q]))
    def skew(k):
        return np.minimum(np.floor(256 * rng.random((N, 8, 16, k)) ** np.exp2(rng.integers(-3, 4, (N, 8, 16, 1)))), 255).astype(np.int64)
    p = skew(P); p[:, :, :3] = rng.integers(0, 256, (N, 8, 3, P))
    return dress(to, rng.integers(0, P, (N, 8, C)), p, skew(C), rng.random((N, 8, C)))
def check_inputs(d):
    bad = []
    for a in ("cells", "pads"):
        v = d[a].astype(np.float32)
        if not ((v >= 0) & (v <= 255) & (v == np.floor(v))).all(): bad.append(a)
    if not ((d["first"] >= 0) & (d["first"] < P)).all(): bad.append("first")
    if not bad and walk(d["cells"], d["first"], d["pads"])[1] > CAP: bad.append("places")
    return bad
def reference(cells, first, pads):
    sent, most = walk(cells, first, pads); y = np.zeros((N, 8, 16, N * CAP), np.float32)
    for r in range(N):
        for q in range(N):
            for g in range(8):
                v = sent[q, r, g][0][:, :CAP]; y[r, g, :, q * CAP:q * CAP + v.shape[1]] = v
    return {"y": y.reshape(N, 128, N * CAP)}

@@ -1,0 +1,292 @@
+from concourse.bass import DstId, RemoteDMATransfer
+from concourse.mybir import AluOpType, ActivationFunctionType
+
+NR, C0, CAP, NP, HOPS = 4, 896, 320, 4096, 3
+HOLD = NR * CAP
+KC = CAP // 16
+DUMP = HOLD + 112
+WIN = DUMP + HOLD
+BIG = 3072.0
+EMPTY = 2048.0
+
+SCRATCH = {
+    "pad": ("sbuf", [128, NP], "bfloat16"),
+    "cel": ("sbuf", [128, C0], "bfloat16"),
+    "fst": ("sbuf", [128, C0 // 16], "int32"),
+    "win0": ("sbuf", [128, WIN], "bfloat16"),
+    "win1": ("sbuf", [128, WIN], "bfloat16"),
+    "win2": ("sbuf", [128, WIN], "bfloat16"),
+    "land0": ("sbuf", [128, 3 * CAP], "bfloat16"),
+    "land1": ("sbuf", [128, 3 * CAP], "bfloat16"),
+    "land2": ("sbuf", [128, 3 * CAP], "bfloat16"),
+    "dd": ("sbuf", [128, HOLD], "bfloat16"),
+    "mm": ("sbuf", [128, HOLD], "bfloat16"),
+    "yy": ("sbuf", [128, HOLD], "float32"),
+    "ia": ("sbuf", [128, 144], "float32"),
+    "ib": ("sbuf", [128, 128], "float32"),
+    "pc": ("sbuf", [128, 8], "int32"),
+    "col": ("sbuf", [128, 8], "float32"),
+    "seld": ("sbuf", [128, 144], "bfloat16"),
+    "selk": ("sbuf", [128, 144], "bfloat16"),
+    "ones": ("sbuf", [128, 128], "bfloat16"),
+    "upp": ("sbuf", [128, 128], "bfloat16"),
+    "ta": ("sbuf", [128, 128], "bfloat16"),
+    "tb": ("sbuf", [128, 128], "bfloat16"),
+    "tc": ("sbuf", [128, 128], "bfloat16"),
+    "rst": ("sbuf", [128, 4 * 80], "float32"),
+    "ki": ("sbuf", [128, 80], "int32"),
+    "kj": ("sbuf", [128, 80], "int32"),
+    "key": ("sbuf", [128, 80], "uint16"),
+    "di": ("sbuf", [128, 80], "int32"),
+    "dj": ("sbuf", [128, 80], "int32"),
+    "oh": ("sbuf", [128, 4 * 80], "bfloat16"),
+    "cum": ("sbuf", [128, 4 * 80], "bfloat16"),
+    "sel": ("sbuf", [128, 4 * 80], "float32"),
+    "off": ("sbuf", [128, 80], "uint16"),
+    "pk0": ("psum", [128, 512], "float32"),
+    "pk1": ("psum", [128, 512], "float32"),
+    "pk2": ("psum", [128, 512], "float32"),
+    "pdst": ("psum", [128, 512], "float32"),
+    "ppre": ("psum", [128, 512], "float32"),
+}
+SEMAPHORES = (["ldp", "ldf", "ldc", "gi", "v", "k0", "k1", "k2", "pd", "pp", "snd", "fwd", "cs", "st", "st2"]
+              + ["%s%d" % (n, h) for n in ("dir", "la", "lb", "rel") for h in range(HOPS)])
+
+
+def routes(T, topo):
+    plan = []
+    for r, src in enumerate(T.cores):
+        direct, relay = [], {}
+        for q, dst in enumerate(T.cores):
+            if q == r:
+                continue
+            if topo.may_write(src, dst):
+                direct.append(q)
+                continue
+            same_die = topo.host(src) == topo.host(dst)
+            cand = [c for c in topo.cores_of(src)
+                    if c not in T.cores and c not in relay.values() and topo.may_write(c, dst)]
+            want = [c for c in cand if (topo.die(c) == topo.die(src)) == same_die]
+            relay[q] = (want or cand)[0]
+        plan.append((direct, relay))
+    return plan
+
+
+def mask_of(engines):
+    m = 0
+    for e in engines:
+        m |= 1 << e
+    return m
+
+
+def late_of(plan, q):
+    return [r for r in range(NR) if q in plan[r][1]]
+
+
+def relay_program(g, core, T, topo, plan, src, dst):
+    lands = [T.land0, T.land1, T.land2]
+    i = late_of(plan, dst).index(src)
+    legs = len(plan[src][1])
+    n_in = len(topo.engines(T.cores[src], core)[0::legs])
+    rid, pid = topo.addr(T.cores[dst], core)
+    n_out = len(topo.engines(core, T.cores[dst]))
+    for h in range(HOPS):
+        g.wait_ge(T.sem["rel%d" % h], n_in)
+        name = "lb%d" % h if (i == 1 and h == HOPS - 1) else "la%d" % h
+        g.remote_dma(lands[h][:, (1 + i) * CAP:(2 + i) * CAP], lands[h][:, 0:CAP], T.sem[name], T.sem.fwd, pid, rid,
+                     topo.mask(core, T.cores[dst]))
+    g.wait_ge(T.sem.fwd, HOPS * n_out)
+
+
+def rank_program(g, core, T, topo):
+    plan = routes(T, topo)
+    rank = T.rank_of(core)
+    if rank is None:
+        for r in range(NR):
+            for q, c in plan[r][1].items():
+                if c == core:
+                    relay_program(g, core, T, topo, plan, r, q)
+        return
+
+    A = AluOpType
+    V, PE, S, SY = g.vector, g.tensor, g.scalar, g.sync
+    sem = T.sem
+    wins = [T.win0, T.win1, T.win2]
+    lands = [T.land0, T.land1, T.land2]
+    direct = plan[rank][0][0]
+    relay = plan[rank][1]
+    late = late_of(plan, rank)
+    n_dir = len(topo.engines(T.cores[direct], core))
+    n_late = [len(topo.engines(plan[r][1][rank], core)) for r in late]
+    cnt = {"v": 0, "k0": 0, "k1": 0, "k2": 0, "pd": 0, "pp": 0, "snd": 0, "st": 0}
+
+    def done(ins, name="v", n=1):
+        ins.then_inc(sem[name], n)
+        cnt[name] += n
+
+    def vw():
+        V.wait_ge(sem.v, cnt["v"])
+
+    SY.dma_start(T.pad[:], T.pads[:]).then_inc(sem.ldp, 16)
+    S.dma_start(T.fst[:], T.first[:]).then_inc(sem.ldf, 16)
+    S.dma_start(T.cel[:], T.cells[:]).then_inc(sem.ldc, 16)
+
+    g.iota(T.pc[:, 0:1], [[1, 1]], 0, 1).then_inc(sem.gi, 1)
+    g.iota(T.ia[:], [[1, 144]], -15, -1, allow_small_or_imprecise_dtypes=True).then_inc(sem.gi, 1)
+    g.iota(T.ib[:], [[16, 8], [0, 16]], 0, -1, allow_small_or_imprecise_dtypes=True).then_inc(sem.gi, 1)
+    g.iota(T.rst[:], [[-16, 80], [20000, 4]], int(BIG), -1, allow_small_or_imprecise_dtypes=True).then_inc(sem.gi, 1)
+    done(V.memset(wins[0][:, DUMP:WIN], EMPTY))
+    V.wait_ge(sem.gi, 4)
+    done(V.tensor_scalar(T.pc[:, 1:2], T.pc[:, 0:1], 15, None, A.bitwise_and))
+    done(V.tensor_scalar(T.ta[:], T.ia[:, 15:143], 0.0, -1.0, A.is_lt, A.mult))
+    done(V.tensor_scalar(T.tb[:], T.ia[:, 15:143], 0.0, BIG, A.is_equal, A.mult))
+    vw()
+    done(V.tensor_scalar(T.col[:, 0:1], T.pc[:, 1:2], -1.0, None, A.mult))
+    done(V.tensor_scalar(T.col[:, 1:2], T.pc[:, 1:2], 0.0, -1.0, A.is_equal, A.mult))
+    done(V.tensor_scalar(T.col[:, 2:3], T.pc[:, 1:2], 1.0, -1.0, A.is_equal, A.mult))
+    done(V.tensor_scalar(T.col[:, 3:4], T.pc[:, 1:2], 2.0, -256.0, A.is_equal, A.mult))
+    done(V.tensor_tensor(T.tc[:], T.ta[:], T.tb[:], A.add))
+    vw()
+    done(V.tensor_tensor(T.col[:, 4:5], T.col[:, 2:3], T.col[:, 3:4], A.add))
+    done(V.tensor_scalar(T.seld[:], T.ia[:], T.col[:, 0:1], T.col[:, 1:2], A.is_equal, A.mult))
+    done(V.tensor_scalar(T.ones[:], T.ib[:], T.col[:, 0:1], None, A.is_equal))
+    vw()
+    done(V.tensor_scalar(T.selk[:], T.ia[:], T.col[:, 0:1], T.col[:, 4:5], A.is_equal, A.mult))
+    done(V.tensor_tensor(T.upp[:], T.tc[:], T.ones[:], A.mult))
+    done(V.memset(wins[1][:, DUMP:WIN], EMPTY))
+    V.wait_ge(sem.ldf, 16)
+    done(V.tensor_copy(T.key[:, 0:C0 // 16], T.fst[:]))
+
+    def pick(out, selector, data, a, b, name):
+        for t in range(16):
+            ins = PE.matmul(out, selector[:, 15 - t:143 - t], data[:, a + t:b:16], t == 0, t == 15)
+        done(ins, name)
+
+    def keys(ps, name, k0, k):
+        V.wait_ge(sem[name], cnt[name])
+        done(V.tensor_copy(T.ki[:, k0:k0 + k], ps[:, 0:k]))
+        vw()
+        done(V.tensor_scalar(T.kj[:, k0:k0 + k], T.ki[:, k0:k0 + k], NP - 1, None, A.bitwise_and))
+        vw()
+        done(V.tensor_copy(T.key[:, k0:k0 + k], T.kj[:, k0:k0 + k]))
+        vw()
+
+    def take(a, n, k0, src, op):
+        done(V.tensor_tensor(T.dd[:, a:a + n], T.pad[:, 0:NP].indirect(T.key[:, k0:k0 + n // 16]), src, op))
+
+    def wrap(a, n):
+        done(V.tensor_scalar(T.mm[:, a:a + n], T.dd[:, a:a + n], 0.0, -256.0, A.is_gt, A.mult))
+
+    def route(h, n):
+        k = n // 16
+        V.wait_ge(sem.pd, cnt["pd"])
+        done(V.tensor_scalar(T.di[:, 0:k], T.pdst[:, 0:k], 256.0, None, A.add))
+        vw()
+        done(V.tensor_scalar(T.dj[:, 0:k], T.di[:, 0:k], 4096 + NR - 1, None, A.bitwise_and))
+        vw()
+        for d in range(NR):
+            done(V.tensor_scalar(T.oh[:, d:NR * k:NR], T.dj[:, 0:k], float(d), None, A.is_equal))
+        PE.wait_ge(sem.v, cnt["v"])
+        PE.matmul(T.ppre[:, 0:NR * k], T.upp[:], T.oh[:, 0:NR * k], True, False)
+        vw()
+        for d in range(NR):
+            o = T.oh[:, d:NR * k:NR]
+            done(V.tensor_tensor_scan(T.cum[:, d:NR * k:NR], o, o, float(d * KC), A.add, A.max))
+        PE.wait_ge(sem.v, cnt["v"])
+        done(PE.matmul(T.ppre[:, 0:NR * k], T.ones[:], T.cum[:, 0:NR * k], False, True), "pp")
+        V.wait_ge(sem.pp, cnt["pp"])
+        done(V.tensor_tensor_scan(T.sel[:, 0:NR * k], T.rst[:, 0:NR * k], T.ppre[:, 0:NR * k], 1.0e6, A.min, A.max))
+        vw()
+        done(V.tensor_scalar(T.off[:, 0:k], T.sel[:, NR - 1:NR * k:NR], BIG - (DUMP - 1), None, A.subtract))
+        vw()
+        done(V.tensor_tensor(wins[h][:, 0:WIN].indirect(T.off[:, 0:k]), T.dd[:, 0:n], T.mm[:, 0:n], A.add))
+
+    def slots(h, q):
+        return wins[h][:, DUMP + q * CAP:DUMP + (q + 1) * CAP]
+
+    def send(h):
+        g.wait_ge(sem.v, cnt["v"])
+        legs = []
+        for i, q in enumerate(sorted(relay)):
+            rid, pid = topo.addr(relay[q], core)
+            eng = topo.engines(core, relay[q])[i::len(relay)]
+            legs.append(RemoteDMATransfer(dst_ids=[DstId(rid=rid, pnc=pid)], dma_engine_mask=mask_of(eng),
+                                          remote_sem=sem["rel%d" % h], src=slots(h, q), dst=lands[h][:, 0:CAP]))
+            cnt["snd"] += len(eng)
+        g.remote_dma_fused(legs, local_sem=sem.snd)
+        rid, pid = topo.addr(T.cores[direct], core)
+        g.remote_dma(lands[h][:, 0:CAP], slots(h, direct), sem["dir%d" % h], sem.snd, pid, rid,
+                     topo.mask(core, T.cores[direct]))
+        cnt["snd"] += len(topo.engines(core, T.cores[direct]))
+
+    V.wait_ge(sem.ldc, 16)
+    vw()
+    V.wait_ge(sem.ldp, 16)
+    take(0, C0, 0, T.cel[:], A.subtract)
+    PE.wait_ge(sem.v, cnt["v"])
+    pick(T.pdst[:, 0:C0 // 16], T.seld, T.dd, 0, C0, "pd")
+    vw()
+    wrap(0, C0)
+    route(0, C0)
+    send(0)
+
+    lo, hi = min(late), max(late)
+    for h in range(1, HOPS):
+        w, land = wins[h - 1], lands[h - 1]
+        PE.wait_ge(sem.v, cnt["v"])
+        pick(T.pk0[:, 0:KC], T.selk, w, DUMP + rank * CAP, DUMP + (rank + 1) * CAP, "k0")
+        if h == 1:
+            vw()
+            done(V.memset(wins[2][:, DUMP:WIN], 0.0))
+        keys(T.pk0, "k0", 0, KC)
+        take(rank * CAP, CAP, 0, slots(h - 1, rank), A.add)
+        vw()
+        wrap(rank * CAP, CAP)
+        PE.wait_ge(sem["dir%d" % (h - 1)], n_dir)
+        pick(T.pk1[:, 0:KC], T.selk, land, 0, CAP, "k1")
+        keys(T.pk1, "k1", KC, KC)
+        take(direct * CAP, CAP, KC, land[:, 0:CAP], A.add)
+        early = cnt["v"]
+        vw()
+        wrap(direct * CAP, CAP)
+        PE.wait_ge(sem["la%d" % (h - 1)], sum(n_late))
+        pick(T.pk2[:, 0:2 * KC], T.selk, land, CAP, 3 * CAP, "k2")
+        PE.wait_ge(sem.v, early)
+        for q in range(NR):
+            if q < lo or q > hi:
+                pick(T.pdst[:, q * KC:(q + 1) * KC], T.seld, T.dd, q * CAP, (q + 1) * CAP, "pd")
+        keys(T.pk2, "k2", 2 * KC, 2 * KC)
+        for i, q in enumerate(late):
+            take(q * CAP, CAP, (2 + i) * KC, land[:, (1 + i) * CAP:(2 + i) * CAP], A.add)
+        PE.wait_ge(sem.v, cnt["v"])
+        pick(T.pdst[:, lo * KC:(hi + 1) * KC], T.seld, T.dd, lo * CAP, (hi + 1) * CAP, "pd")
+        vw()
+        for q in late:
+            wrap(q * CAP, CAP)
+        route(h, HOLD)
+        send(h)
+
+    h = HOPS - 1
+    land = lands[h]
+
+    def out(q, src):
+        vw()
+        done(V.tensor_scalar(T.yy[:, q * CAP:(q + 1) * CAP], src, -1.0, None, A.mult))
+        SY.wait_ge(sem.v, cnt["v"])
+        done(SY.dma_start(T.y[:, q * CAP:(q + 1) * CAP], T.yy[:, q * CAP:(q + 1) * CAP]), "st", 16)
+
+    SY.wait_ge(sem.snd, cnt["snd"])
+    out(rank, slots(h, rank))
+    V.wait_ge(sem["dir%d" % h], n_dir)
+    out(direct, land[:, 0:CAP])
+    V.wait_ge(sem["la%d" % h], n_late[0])
+    out(late[0], land[:, CAP:2 * CAP])
+    q = late[1]
+    S.wait_ge(sem["lb%d" % h], n_late[1])
+    S.activation(T.yy[:, q * CAP:(q + 1) * CAP], land[:, 2 * CAP:3 * CAP], ActivationFunctionType.Copy,
+                 scale=-1.0).then_inc(sem.cs, 1)
+    S.wait_ge(sem.cs, 1)
+    S.dma_start(T.y[:, q * CAP:(q + 1) * CAP], T.yy[:, q * CAP:(q + 1) * CAP]).then_inc(sem.st2, 16)
+    S.wait_ge(sem.st2, 16)
+    SY.wait_ge(sem.st, cnt["st"])
+    g.wait_ge(sem.snd, cnt["snd"])

@@ -7,11 +7,14 @@ KC = CAP // 16
 DUMP = HOLD + 112
 WIN = DUMP + HOLD
 BIG = 3072.0
-EMPTY = 2048.0
+EMPTY = -256.0
+NOPAD = 2304.0
+HALF = C0 // 2
+D0 = HALF
 
 SCRATCH = {
-    "pad": ("sbuf", [128, NP], "bfloat16"),
-    "cel": ("sbuf", [128, C0], "bfloat16"),
+    "pad": ("sbuf", [128, NP + 16], "bfloat16"),
+    "cel": ("sbuf", [128, C0 + HALF], "bfloat16"),
     "fst": ("sbuf", [128, C0 // 16], "int32"),
     "win0": ("sbuf", [128, WIN], "bfloat16"),
     "win1": ("sbuf", [128, WIN], "bfloat16"),
@@ -19,7 +22,8 @@ SCRATCH = {
     "land0": ("sbuf", [128, 3 * CAP], "bfloat16"),
     "land1": ("sbuf", [128, 3 * CAP], "bfloat16"),
     "land2": ("sbuf", [128, 3 * CAP], "bfloat16"),
-    "dd": ("sbuf", [128, HOLD], "bfloat16"),
+    "dd": ("sbuf", [128, D0 + HOLD + CAP], "bfloat16"),
+    "selp": ("sbuf", [128, 144], "bfloat16"),
     "mm": ("sbuf", [128, HOLD], "bfloat16"),
     "yy": ("sbuf", [128, HOLD], "float32"),
     "ia": ("sbuf", [128, 144], "float32"),
@@ -37,6 +41,10 @@ SCRATCH = {
     "ki": ("sbuf", [128, 80], "int32"),
     "kj": ("sbuf", [128, 80], "int32"),
     "key": ("sbuf", [128, 80], "uint16"),
+    "ks0": ("sbuf", [128, 64], "uint16"),
+    "ks1": ("sbuf", [128, 64], "uint16"),
+    "kl0": ("sbuf", [128, 48], "uint16"),
+    "kl1": ("sbuf", [128, 48], "uint16"),
     "di": ("sbuf", [128, 80], "int32"),
     "dj": ("sbuf", [128, 80], "int32"),
     "oh": ("sbuf", [128, 4 * 80], "bfloat16"),
@@ -49,14 +57,15 @@ SCRATCH = {
     "pdst": ("psum", [128, 512], "float32"),
     "ppre": ("psum", [128, 512], "float32"),
 }
-SEMAPHORES = (["ldp", "ldf", "ldc", "gi", "v", "k0", "k1", "k2", "pd", "pp", "snd", "fwd", "cs", "st", "st2"]
-              + ["%s%d" % (n, h) for n in ("dir", "la", "lb", "rel") for h in range(HOPS)])
+SEMAPHORES = (["ldp", "ldf", "ldc", "gi", "v", "k0", "k1", "k2", "pd", "pp", "snd", "fwd", "cs", "st", "st2", "sg"]
+              + ["%s%d" % (n, h) for n in ("dir", "la", "lb", "rel") for h in range(HOPS)]
+              + ["%s%d" % (n, h) for n in ("lk", "rek") for h in range(HOPS - 1)])
 
 
 def routes(T, topo):
     plan = []
     for r, src in enumerate(T.cores):
-        direct, relay = [], {}
+        direct, relay, krelay = [], {}, {}
         for q, dst in enumerate(T.cores):
             if q == r:
                 continue
@@ -68,7 +77,12 @@ def routes(T, topo):
                     if c not in T.cores and c not in relay.values() and topo.may_write(c, dst)]
             want = [c for c in cand if (topo.die(c) == topo.die(src)) == same_die]
             relay[q] = (want or cand)[0]
-        plan.append((direct, relay))
+        for q in relay:
+            cand = [c for c in topo.cores_of(src) if c not in T.cores and c not in relay.values()
+                    and c not in krelay.values() and topo.may_write(c, T.cores[q])]
+            want = [c for c in cand if topo.die(c) == topo.die(relay[q])]
+            krelay[q] = (want or cand)[0]
+        plan.append((direct, relay, krelay))
     return plan
 
 
@@ -98,6 +112,18 @@ def relay_program(g, core, T, topo, plan, src, dst):
     g.wait_ge(T.sem.fwd, HOPS * n_out)
 
 
+def key_relay_program(g, core, T, topo, plan, src, dst):
+    kls = [T.kl0, T.kl1]
+    i = late_of(plan, dst).index(src)
+    n_in = len(topo.engines(T.cores[src], core)[0::len(plan[src][2])])
+    rid, pid = topo.addr(T.cores[dst], core)
+    for h in range(HOPS - 1):
+        g.wait_ge(T.sem["rek%d" % h], n_in)
+        g.remote_dma(kls[h][:, i * KC:(i + 1) * KC], kls[h][:, 0:KC], T.sem["lk%d" % h], T.sem.fwd, pid, rid,
+                     topo.mask(core, T.cores[dst]))
+    g.wait_ge(T.sem.fwd, (HOPS - 1) * len(topo.engines(core, T.cores[dst])))
+
+
 def rank_program(g, core, T, topo):
     plan = routes(T, topo)
     rank = T.rank_of(core)
@@ -106,6 +132,9 @@ def rank_program(g, core, T, topo):
             for q, c in plan[r][1].items():
                 if c == core:
                     relay_program(g, core, T, topo, plan, r, q)
+            for q, c in plan[r][2].items():
+                if c == core:
+                    key_relay_program(g, core, T, topo, plan, r, q)
         return
 
     A = AluOpType
@@ -118,7 +147,11 @@ def rank_program(g, core, T, topo):
     late = late_of(plan, rank)
     n_dir = len(topo.engines(T.cores[direct], core))
     n_late = [len(topo.engines(plan[r][1][rank], core)) for r in late]
-    cnt = {"v": 0, "k0": 0, "k1": 0, "k2": 0, "pd": 0, "pp": 0, "snd": 0, "st": 0}
+    krelay = plan[rank][2]
+    n_lk = sum(len(topo.engines(plan[r][2][rank], core)) for r in late)
+    kss, kls = [T.ks0, T.ks1], [T.kl0, T.kl1]
+    block = {q: i for i, q in enumerate(sorted(relay) + [rank, direct])}
+    cnt = {"v": 0, "k0": 0, "k1": 0, "k2": 0, "pd": 0, "pp": 0, "snd": 0, "st": 0, "sg": 0}
 
     def done(ins, name="v", n=1):
         ins.then_inc(sem[name], n)
@@ -127,15 +160,17 @@ def rank_program(g, core, T, topo):
     def vw():
         V.wait_ge(sem.v, cnt["v"])
 
-    SY.dma_start(T.pad[:], T.pads[:]).then_inc(sem.ldp, 16)
+    SY.dma_start(T.pad[:, 0:NP], T.pads[:]).then_inc(sem.ldp, 16)
     S.dma_start(T.fst[:], T.first[:]).then_inc(sem.ldf, 16)
-    S.dma_start(T.cel[:], T.cells[:]).then_inc(sem.ldc, 16)
+    S.dma_start(T.cel[:, 0:C0], T.cells[:]).then_inc(sem.ldc, 16)
 
     g.iota(T.pc[:, 0:1], [[1, 1]], 0, 1).then_inc(sem.gi, 1)
     g.iota(T.ia[:], [[1, 144]], -15, -1, allow_small_or_imprecise_dtypes=True).then_inc(sem.gi, 1)
     g.iota(T.ib[:], [[16, 8], [0, 16]], 0, -1, allow_small_or_imprecise_dtypes=True).then_inc(sem.gi, 1)
     g.iota(T.rst[:], [[-16, 80], [20000, 4]], int(BIG), -1, allow_small_or_imprecise_dtypes=True).then_inc(sem.gi, 1)
     done(V.memset(wins[0][:, DUMP:WIN], EMPTY))
+    done(V.memset(T.pad[:, NP:NP + 16], NOPAD))
+    done(V.memset(T.cel[:, C0:C0 + HALF], 0.0))
     V.wait_ge(sem.gi, 4)
     done(V.tensor_scalar(T.pc[:, 1:2], T.pc[:, 0:1], 15, None, A.bitwise_and))
     done(V.tensor_scalar(T.ta[:], T.ia[:, 15:143], 0.0, -1.0, A.is_lt, A.mult))
@@ -153,34 +188,44 @@ def rank_program(g, core, T, topo):
     vw()
     done(V.tensor_scalar(T.selk[:], T.ia[:], T.col[:, 0:1], T.col[:, 4:5], A.is_equal, A.mult))
     done(V.tensor_tensor(T.upp[:], T.tc[:], T.ones[:], A.mult))
+    done(V.tensor_scalar(T.selp[:], T.seld[:], -1.0, None, A.mult))
     done(V.memset(wins[1][:, DUMP:WIN], EMPTY))
     V.wait_ge(sem.ldf, 16)
     done(V.tensor_copy(T.key[:, 0:C0 // 16], T.fst[:]))
 
-    def pick(out, selector, data, a, b, name):
+    def pick(out, selector, data, a, b, name, start=True, stop=True):
         for t in range(16):
-            ins = PE.matmul(out, selector[:, 15 - t:143 - t], data[:, a + t:b:16], t == 0, t == 15)
-        done(ins, name)
+            ins = PE.matmul(out, selector[:, 15 - t:143 - t], data[:, a + t:b:16], start and t == 0, stop and t == 15)
+        if stop:
+            done(ins, name)
 
-    def keys(ps, name, k0, k):
+    def keys(ps, name, out, k):
         V.wait_ge(sem[name], cnt[name])
-        done(V.tensor_copy(T.ki[:, k0:k0 + k], ps[:, 0:k]))
         vw()
-        done(V.tensor_scalar(T.kj[:, k0:k0 + k], T.ki[:, k0:k0 + k], NP - 1, None, A.bitwise_and))
+        done(V.tensor_copy(T.ki[:, 0:k], ps[:, 0:k]))
         vw()
-        done(V.tensor_copy(T.key[:, k0:k0 + k], T.kj[:, k0:k0 + k]))
+        done(V.tensor_scalar(T.kj[:, 0:k], T.ki[:, 0:k], 65536 + NP - 1, None, A.bitwise_and))
         vw()
+        done(V.tensor_scalar(out, T.kj[:, 0:k], float(NP), None, A.min))
 
-    def take(a, n, k0, src, op):
-        done(V.tensor_tensor(T.dd[:, a:a + n], T.pad[:, 0:NP].indirect(T.key[:, k0:k0 + n // 16]), src, op))
+    def take(a, n, key, src, op):
+        done(V.tensor_tensor(T.dd[:, D0 + a:D0 + a + n], T.pad[:].indirect(key), src, op))
+
+    def peek(a, n, key, bias):
+        done(S.activation(T.dd[:, D0 + a:D0 + a + n], T.pad[:].indirect(key), ActivationFunctionType.Identity,
+                          bias=bias), "sg")
 
     def wrap(a, n):
-        done(V.tensor_scalar(T.mm[:, a:a + n], T.dd[:, a:a + n], 0.0, -256.0, A.is_gt, A.mult))
+        done(V.tensor_scalar(T.mm[:, a:a + n], T.dd[:, D0 + a:D0 + a + n], 0.0, -256.0, A.is_gt, A.mult))
 
-    def route(h, n):
+    def symbol0(ps, a, k0, k):
+        done(V.tensor_scalar(T.di[:, k0:k0 + k], ps[:, a:a + k], 256.0, None, A.add))
+
+    def route(h, n, parts):
         k = n // 16
         V.wait_ge(sem.pd, cnt["pd"])
-        done(V.tensor_scalar(T.di[:, 0:k], T.pdst[:, 0:k], 256.0, None, A.add))
+        for part in parts:
+            symbol0(T.pdst, *part)
         vw()
         done(V.tensor_scalar(T.dj[:, 0:k], T.di[:, 0:k], 4096 + NR - 1, None, A.bitwise_and))
         vw()
@@ -191,7 +236,7 @@ def rank_program(g, core, T, topo):
         vw()
         for d in range(NR):
             o = T.oh[:, d:NR * k:NR]
-            done(V.tensor_tensor_scan(T.cum[:, d:NR * k:NR], o, o, float(d * KC), A.add, A.max))
+            done(V.tensor_tensor_scan(T.cum[:, d:NR * k:NR], o, o, float(block[d] * KC), A.add, A.max))
         PE.wait_ge(sem.v, cnt["v"])
         done(PE.matmul(T.ppre[:, 0:NR * k], T.ones[:], T.cum[:, 0:NR * k], False, True), "pp")
         V.wait_ge(sem.pp, cnt["pp"])
@@ -199,10 +244,22 @@ def rank_program(g, core, T, topo):
         vw()
         done(V.tensor_scalar(T.off[:, 0:k], T.sel[:, NR - 1:NR * k:NR], BIG - (DUMP - 1), None, A.subtract))
         vw()
-        done(V.tensor_tensor(wins[h][:, 0:WIN].indirect(T.off[:, 0:k]), T.dd[:, 0:n], T.mm[:, 0:n], A.add))
+        done(V.tensor_tensor(wins[h][:, 0:WIN].indirect(T.off[:, 0:k]), T.dd[:, D0:D0 + n], T.mm[:, 0:n], A.add))
 
     def slots(h, q):
-        return wins[h][:, DUMP + q * CAP:DUMP + (q + 1) * CAP]
+        return wins[h][:, DUMP + block[q] * CAP:DUMP + (block[q] + 1) * CAP]
+
+    def send_keys(h):
+        g.wait_ge(sem.v, cnt["v"])
+        legs = []
+        for i, q in enumerate(sorted(krelay)):
+            rid, pid = topo.addr(krelay[q], core)
+            eng = topo.engines(core, krelay[q])[i::len(krelay)]
+            legs.append(RemoteDMATransfer(dst_ids=[DstId(rid=rid, pnc=pid)], dma_engine_mask=mask_of(eng),
+                                          remote_sem=sem["rek%d" % h], src=kss[h][:, i * KC:(i + 1) * KC],
+                                          dst=kls[h][:, 0:KC]))
+            cnt["snd"] += len(eng)
+        g.remote_dma_fused(legs, local_sem=sem.snd)
 
     def send(h):
         g.wait_ge(sem.v, cnt["v"])
@@ -219,51 +276,76 @@ def rank_program(g, core, T, topo):
                      topo.mask(core, T.cores[direct]))
         cnt["snd"] += len(topo.engines(core, T.cores[direct]))
 
+    kh = HALF // 16
+    PE.wait_ge(sem.v, cnt["v"])
+    PE.wait_ge(sem.ldc, 16)
+    pick(T.pdst[:, 0:2 * kh], T.selp, T.cel, HALF, 3 * HALF, "pd", True, False)
+    S.wait_ge(sem.v, cnt["v"])
+    S.wait_ge(sem.ldp, 16)
+    peek(-HALF, HALF, T.key[:, kh:2 * kh], 0.0)
     V.wait_ge(sem.ldc, 16)
     vw()
     V.wait_ge(sem.ldp, 16)
-    take(0, C0, 0, T.cel[:], A.subtract)
+    take(0, HALF, T.key[:, 0:kh], T.cel[:, 0:HALF], A.subtract)
     PE.wait_ge(sem.v, cnt["v"])
-    pick(T.pdst[:, 0:C0 // 16], T.seld, T.dd, 0, C0, "pd")
+    PE.wait_ge(sem.sg, cnt["sg"])
+    pick(T.pdst[:, 0:2 * kh], T.seld, T.dd, 0, C0, "pd", False, True)
+    take(HALF, HALF, T.key[:, kh:2 * kh], T.cel[:, HALF:C0], A.subtract)
     vw()
     wrap(0, C0)
-    route(0, C0)
+    route(0, C0, [(0, kh, kh), (kh, 0, kh)])
     send(0)
 
-    lo, hi = min(late), max(late)
+    near = direct ^ 1
+    far = [q for q in late if q != near][0]
+    pair = min(near, direct)
+    spare = -CAP if pair == 0 else HOLD
+    p0 = min(spare, pair * CAP)
+    parts = [((spare - p0) // 16, far * KC, KC), ((pair * CAP - p0) // 16, pair * KC, 2 * KC)]
     for h in range(1, HOPS):
+        S.wait_ge(sem.v, cnt["v"])
         w, land = wins[h - 1], lands[h - 1]
         PE.wait_ge(sem.v, cnt["v"])
-        pick(T.pk0[:, 0:KC], T.selk, w, DUMP + rank * CAP, DUMP + (rank + 1) * CAP, "k0")
+        pick(T.pk0[:, 0:3 * KC], T.selk, w, DUMP, DUMP + 3 * CAP, "k0")
         if h == 1:
             vw()
             done(V.memset(wins[2][:, DUMP:WIN], 0.0))
-        keys(T.pk0, "k0", 0, KC)
-        take(rank * CAP, CAP, 0, slots(h - 1, rank), A.add)
+        keys(T.pk0, "k0", kss[h - 1][:, 0:3 * KC], 3 * KC)
+        send_keys(h - 1)
+        vw()
+        take(rank * CAP, CAP, kss[h - 1][:, 2 * KC:3 * KC], slots(h - 1, rank), A.add)
+        own = cnt["v"]
         vw()
         wrap(rank * CAP, CAP)
         PE.wait_ge(sem["dir%d" % (h - 1)], n_dir)
         pick(T.pk1[:, 0:KC], T.selk, land, 0, CAP, "k1")
-        keys(T.pk1, "k1", KC, KC)
-        take(direct * CAP, CAP, KC, land[:, 0:CAP], A.add)
-        early = cnt["v"]
+        PE.wait_ge(sem.v, own)
+        pick(T.pk2[:, 0:KC], T.seld, T.dd, D0 + rank * CAP, D0 + (rank + 1) * CAP, "k2")
+        keys(T.pk1, "k1", T.key[:, 0:KC], KC)
+        vw()
+        take(direct * CAP, CAP, T.key[:, 0:KC], land[:, 0:CAP], A.add)
         vw()
         wrap(direct * CAP, CAP)
-        PE.wait_ge(sem["la%d" % (h - 1)], sum(n_late))
-        pick(T.pk2[:, 0:2 * KC], T.selk, land, CAP, 3 * CAP, "k2")
-        PE.wait_ge(sem.v, early)
-        for q in range(NR):
-            if q < lo or q > hi:
-                pick(T.pdst[:, q * KC:(q + 1) * KC], T.seld, T.dd, q * CAP, (q + 1) * CAP, "pd")
-        keys(T.pk2, "k2", 2 * KC, 2 * KC)
-        for i, q in enumerate(late):
-            take(q * CAP, CAP, (2 + i) * KC, land[:, (1 + i) * CAP:(2 + i) * CAP], A.add)
-        PE.wait_ge(sem.v, cnt["v"])
-        pick(T.pdst[:, lo * KC:(hi + 1) * KC], T.seld, T.dd, lo * CAP, (hi + 1) * CAP, "pd")
+        V.wait_ge(sem.k2, cnt["k2"])
+        symbol0(T.pk2, 0, rank * KC, KC)
+        S.wait_ge(sem["lk%d" % (h - 1)], n_lk)
+        i = late.index(far)
+        peek(spare, CAP, kls[h - 1][:, i * KC:(i + 1) * KC], float(-rank))
+        V.wait_ge(sem["la%d" % (h - 1)], sum(n_late))
+        V.wait_ge(sem["lk%d" % (h - 1)], n_lk)
+        for q in (near, far):
+            i = late.index(q)
+            take(q * CAP, CAP, kls[h - 1][:, i * KC:(i + 1) * KC], land[:, (1 + i) * CAP:(2 + i) * CAP], A.add)
+            if q == near:
+                first = cnt["v"]
+                PE.wait_ge(sem.v, first)
+                PE.wait_ge(sem.sg, cnt["sg"])
+                pick(T.pdst[:, 0:3 * KC], T.seld, T.dd, D0 + p0, D0 + p0 + 3 * CAP, "pd")
+        V.wait_ge(sem.v, first)
+        wrap(near * CAP, CAP)
         vw()
-        for q in late:
-            wrap(q * CAP, CAP)
-        route(h, HOLD)
+        wrap(far * CAP, CAP)
+        route(h, HOLD, parts)
         send(h)
 
     h = HOPS - 1

@@ -11,9 +11,16 @@ EMPTY = -256.0
 NOPAD = 2304.0
 HALF = C0 // 2
 D0 = HALF
+SEG = NP // 16
+TAKE, KEEP = 1.0e6, 131072.0
 
 SCRATCH = {
     "pad": ("sbuf", [128, NP + 16], "bfloat16"),
+    "tab": ("sbuf", [128, NP + 16], "bfloat16"),
+    "row": ("sbuf", [128, SEG], "bfloat16"),
+    "rwi": ("sbuf", [128, SEG], "int32"),
+    "rwj": ("sbuf", [128, SEG], "int32"),
+    "rwd": ("sbuf", [128, SEG], "bfloat16"),
     "cel": ("sbuf", [128, C0 + HALF], "bfloat16"),
     "fst": ("sbuf", [128, C0 // 16], "int32"),
     "win0": ("sbuf", [128, WIN], "bfloat16"),
@@ -22,31 +29,23 @@ SCRATCH = {
     "land0": ("sbuf", [128, 3 * CAP], "bfloat16"),
     "land1": ("sbuf", [128, 3 * CAP], "bfloat16"),
     "land2": ("sbuf", [128, 3 * CAP], "bfloat16"),
-    "dd": ("sbuf", [128, D0 + HOLD + CAP], "bfloat16"),
-    "selp": ("sbuf", [128, 144], "bfloat16"),
+    "dd": ("sbuf", [128, D0 + HOLD], "bfloat16"),
+    "dst": ("sbuf", [128, HOLD], "bfloat16"),
     "mm": ("sbuf", [128, HOLD], "bfloat16"),
     "yy": ("sbuf", [128, HOLD], "float32"),
-    "ia": ("sbuf", [128, 144], "float32"),
-    "ib": ("sbuf", [128, 128], "float32"),
     "pc": ("sbuf", [128, 8], "int32"),
     "col": ("sbuf", [128, 8], "float32"),
-    "seld": ("sbuf", [128, 144], "bfloat16"),
-    "selk": ("sbuf", [128, 144], "bfloat16"),
+    "sels": ("sbuf", [128, 640], "bfloat16"),
     "ones": ("sbuf", [128, 128], "bfloat16"),
     "upp": ("sbuf", [128, 128], "bfloat16"),
-    "ta": ("sbuf", [128, 128], "bfloat16"),
-    "tb": ("sbuf", [128, 128], "bfloat16"),
-    "tc": ("sbuf", [128, 128], "bfloat16"),
     "rst": ("sbuf", [128, 4 * 80], "float32"),
     "ki": ("sbuf", [128, 80], "int32"),
     "kj": ("sbuf", [128, 80], "int32"),
     "key": ("sbuf", [128, 80], "uint16"),
     "ks0": ("sbuf", [128, 64], "uint16"),
     "ks1": ("sbuf", [128, 64], "uint16"),
-    "kl0": ("sbuf", [128, 48], "uint16"),
-    "kl1": ("sbuf", [128, 48], "uint16"),
-    "di": ("sbuf", [128, 80], "int32"),
-    "dj": ("sbuf", [128, 80], "int32"),
+    "kl0": ("sbuf", [128, 64], "uint16"),
+    "kl1": ("sbuf", [128, 64], "uint16"),
     "oh": ("sbuf", [128, 4 * 80], "bfloat16"),
     "cum": ("sbuf", [128, 4 * 80], "bfloat16"),
     "sel": ("sbuf", [128, 4 * 80], "float32"),
@@ -54,10 +53,11 @@ SCRATCH = {
     "pk0": ("psum", [128, 512], "float32"),
     "pk1": ("psum", [128, 512], "float32"),
     "pk2": ("psum", [128, 512], "float32"),
+    "alt": ("sbuf", [128, 80], "float32"),
     "pdst": ("psum", [128, 512], "float32"),
     "ppre": ("psum", [128, 512], "float32"),
 }
-SEMAPHORES = (["ldp", "ldf", "ldc", "gi", "v", "k0", "k1", "k2", "pd", "pp", "snd", "fwd", "cs", "st", "st2", "sg"]
+SEMAPHORES = (["ldp", "ldf", "ldc", "ldr", "ldt", "gi", "v", "k0", "k1", "k2", "pd", "pp", "snd", "fwd", "cs", "st", "st2", "sg"]
               + ["%s%d" % (n, h) for n in ("dir", "la", "lb", "rel") for h in range(HOPS)]
               + ["%s%d" % (n, h) for n in ("lk", "rek") for h in range(HOPS - 1)])
 
@@ -97,16 +97,30 @@ def late_of(plan, q):
     return [r for r in range(NR) if q in plan[r][1]]
 
 
+def key_engines(T, topo, plan, src, dst):
+    krelay = plan[src][2]
+    return topo.engines(T.cores[src], krelay[dst])[sorted(krelay).index(dst)::len(krelay)]
+
+
+def cell_engines(T, topo, plan, src, dst, h):
+    direct, relay, _ = plan[src]
+    out = topo.engines(T.cores[src], T.cores[direct[0]])
+    if dst not in relay:
+        return out
+    every = topo.engines(T.cores[src], relay[dst])
+    if h == HOPS - 1:
+        return every[sorted(relay).index(dst)::len(relay)]
+    return [e for e in every if e not in out]
+
+
 def relay_program(g, core, T, topo, plan, src, dst):
     lands = [T.land0, T.land1, T.land2]
     i = late_of(plan, dst).index(src)
-    legs = len(plan[src][1])
-    n_in = len(topo.engines(T.cores[src], core)[0::legs])
     rid, pid = topo.addr(T.cores[dst], core)
     n_out = len(topo.engines(core, T.cores[dst]))
     for h in range(HOPS):
-        g.wait_ge(T.sem["rel%d" % h], n_in)
-        name = "lb%d" % h if (i == 1 and h == HOPS - 1) else "la%d" % h
+        g.wait_ge(T.sem["rel%d" % h], len(cell_engines(T, topo, plan, src, dst, h)))
+        name = ("la%d", "lb%d")[i] % h
         g.remote_dma(lands[h][:, (1 + i) * CAP:(2 + i) * CAP], lands[h][:, 0:CAP], T.sem[name], T.sem.fwd, pid, rid,
                      topo.mask(core, T.cores[dst]))
     g.wait_ge(T.sem.fwd, HOPS * n_out)
@@ -115,7 +129,7 @@ def relay_program(g, core, T, topo, plan, src, dst):
 def key_relay_program(g, core, T, topo, plan, src, dst):
     kls = [T.kl0, T.kl1]
     i = late_of(plan, dst).index(src)
-    n_in = len(topo.engines(T.cores[src], core)[0::len(plan[src][2])])
+    n_in = len(key_engines(T, topo, plan, src, dst))
     rid, pid = topo.addr(T.cores[dst], core)
     for h in range(HOPS - 1):
         g.wait_ge(T.sem["rek%d" % h], n_in)
@@ -137,7 +151,7 @@ def rank_program(g, core, T, topo):
                     key_relay_program(g, core, T, topo, plan, r, q)
         return
 
-    A = AluOpType
+    A, F = AluOpType, ActivationFunctionType
     V, PE, S, SY = g.vector, g.tensor, g.scalar, g.sync
     sem = T.sem
     wins = [T.win0, T.win1, T.win2]
@@ -151,7 +165,8 @@ def rank_program(g, core, T, topo):
     n_lk = sum(len(topo.engines(plan[r][2][rank], core)) for r in late)
     kss, kls = [T.ks0, T.ks1], [T.kl0, T.kl1]
     block = {q: i for i, q in enumerate(sorted(relay) + [rank, direct])}
-    cnt = {"v": 0, "k0": 0, "k1": 0, "k2": 0, "pd": 0, "pp": 0, "snd": 0, "st": 0, "sg": 0}
+    turn = sorted(late, key=lambda q: topo.host(T.cores[q]) != topo.host(core))
+    cnt = {"v": 0, "k0": 0, "k1": 0, "k2": 0, "pd": 0, "pp": 0, "snd": 0, "st": 0, "sg": 0, "gi": 0}
 
     def done(ins, name="v", n=1):
         ins.then_inc(sem[name], n)
@@ -160,49 +175,68 @@ def rank_program(g, core, T, topo):
     def vw():
         V.wait_ge(sem.v, cnt["v"])
 
-    SY.dma_start(T.pad[:, 0:NP], T.pads[:]).then_inc(sem.ldp, 16)
     S.dma_start(T.fst[:], T.first[:]).then_inc(sem.ldf, 16)
-    S.dma_start(T.cel[:, 0:C0], T.cells[:]).then_inc(sem.ldc, 16)
+    SY.dma_start(T.cel[:, 0:C0], T.cells[:]).then_inc(sem.ldc, 16)
+    SY.dma_start(T.pad[:, 0:NP], T.pads[:]).then_inc(sem.ldp, 16)
+    SY.dma_start(T.row[:], T.pads[0:128:16, :]).then_inc(sem.ldr, 16)
 
-    g.iota(T.pc[:, 0:1], [[1, 1]], 0, 1).then_inc(sem.gi, 1)
-    g.iota(T.ia[:], [[1, 144]], -15, -1, allow_small_or_imprecise_dtypes=True).then_inc(sem.gi, 1)
-    g.iota(T.ib[:], [[16, 8], [0, 16]], 0, -1, allow_small_or_imprecise_dtypes=True).then_inc(sem.gi, 1)
-    g.iota(T.rst[:], [[-16, 80], [20000, 4]], int(BIG), -1, allow_small_or_imprecise_dtypes=True).then_inc(sem.gi, 1)
-    done(V.memset(wins[0][:, DUMP:WIN], EMPTY))
-    done(V.memset(T.pad[:, NP:NP + 16], NOPAD))
+    selp, seld, selk, selq = 0, 160, 320, 480
+    done(V.memset(T.sels[:], 0.0))
+    done(V.memset(T.upp[:], -1.0))
+    done(V.memset(T.ones[:], 1.0))
+    filled = cnt["v"]
     done(V.memset(T.cel[:, C0:C0 + HALF], 0.0))
-    V.wait_ge(sem.gi, 4)
+    done(V.memset(T.pad[:, NP:NP + 16], NOPAD))
+    done(V.memset(T.alt[:], -TAKE))
+    done(V.memset(wins[0][:, DUMP:WIN], EMPTY))
+
+    def mark(ap, pattern, op, fill, base, by):
+        done(g.affine_select(ap, ap, pattern, op, fill, base, by), "gi")
+        return cnt["gi"]
+
+    def weight(ap, pattern, symbol, w):
+        return mark(ap, pattern, A.not_equal, w, symbol - 1000 * (pattern[-1][1] - 1), -1)
+
+    one, four = [[16, 9], [1000, 16]], [[16, 9], [0, 4], [1000, 4]]
+    done(g.iota(T.pc[:, 0:1], [[1, 1]], 0, 1), "gi")
+    g.wait_ge(sem.v, filled)
+    made_p = weight(T.sels[:, 0:144], one, 0, 1.0)
+    made_d = weight(T.sels[:, 160:304], one, 0, -1.0)
+    mark(T.upp[:], [[-1, 128]], A.is_gt, 0.0, 0, 1)
+    g.wait_ge(sem.gi, mark(T.ones[:], [[-16, 8], [0, 16]], A.is_ge, 0.0, 0, 1))
+    mark(T.upp[:], [[16, 8], [0, 16]], A.is_ge, 0.0, 15, -1)
+    g.wait_ge(sem.gi, mark(T.ones[:], [[16, 8], [0, 16]], A.is_ge, 0.0, 15, -1))
+    made_u = mark(T.upp[:], [[-1, 128]], A.not_equal, BIG, 0, 1)
+    done(g.iota(T.rst[:], [[-16, 80], [20000, 4]], int(BIG), -1, allow_small_or_imprecise_dtypes=True), "gi")
+    made_r = cnt["gi"]
+    weight(T.sels[:, 320:464], one, 1, -1.0)
+    g.wait_ge(sem.gi, weight(T.sels[:, 492:636], four, 1, -1.0))
+    weight(T.sels[:, 320:464], one, 2, -256.0)
+    made_k = weight(T.sels[:, 492:636], four, 2, -256.0)
+
+    V.wait_ge(sem.gi, 1)
     done(V.tensor_scalar(T.pc[:, 1:2], T.pc[:, 0:1], 15, None, A.bitwise_and))
-    done(V.tensor_scalar(T.ta[:], T.ia[:, 15:143], 0.0, -1.0, A.is_lt, A.mult))
-    done(V.tensor_scalar(T.tb[:], T.ia[:, 15:143], 0.0, BIG, A.is_equal, A.mult))
     vw()
-    done(V.tensor_scalar(T.col[:, 0:1], T.pc[:, 1:2], -1.0, None, A.mult))
-    done(V.tensor_scalar(T.col[:, 1:2], T.pc[:, 1:2], 0.0, -1.0, A.is_equal, A.mult))
-    done(V.tensor_scalar(T.col[:, 2:3], T.pc[:, 1:2], 1.0, -1.0, A.is_equal, A.mult))
-    done(V.tensor_scalar(T.col[:, 3:4], T.pc[:, 1:2], 2.0, -256.0, A.is_equal, A.mult))
-    done(V.tensor_tensor(T.tc[:], T.ta[:], T.tb[:], A.add))
+    for i in (1, 2, 3):
+        done(V.tensor_scalar(T.col[:, i:i + 1], T.pc[:, 1:2], 4.0 * i, TAKE + KEEP, A.is_lt, A.mult))
     vw()
-    done(V.tensor_tensor(T.col[:, 4:5], T.col[:, 2:3], T.col[:, 3:4], A.add))
-    done(V.tensor_scalar(T.seld[:], T.ia[:], T.col[:, 0:1], T.col[:, 1:2], A.is_equal, A.mult))
-    done(V.tensor_scalar(T.ones[:], T.ib[:], T.col[:, 0:1], None, A.is_equal))
-    vw()
-    done(V.tensor_scalar(T.selk[:], T.ia[:], T.col[:, 0:1], T.col[:, 4:5], A.is_equal, A.mult))
-    done(V.tensor_tensor(T.upp[:], T.tc[:], T.ones[:], A.mult))
-    done(V.tensor_scalar(T.selp[:], T.seld[:], -1.0, None, A.mult))
-    done(V.memset(wins[1][:, DUMP:WIN], EMPTY))
+    for i in (1, 2, 3):
+        done(V.tensor_scalar(T.alt[:, i:4 * KC:4], T.alt[:, i:4 * KC:4], T.col[:, i:i + 1], None, A.add))
     V.wait_ge(sem.ldf, 16)
     done(V.tensor_copy(T.key[:, 0:C0 // 16], T.fst[:]))
+    ready = cnt["v"]
 
-    def pick(out, selector, data, a, b, name, start=True, stop=True):
-        for t in range(16):
-            ins = PE.matmul(out, selector[:, 15 - t:143 - t], data[:, a + t:b:16], start and t == 0, stop and t == 15)
+    def pick(out, sel, data, a, b, name, start=True, stop=True, m=16):
+        for t in range(m):
+            ins = PE.matmul(out, T.sels[:, sel + 15 - t:sel + 143 - t], data[:, a + t:b:m], start and t == 0,
+                            stop and t == m - 1)
         if stop:
             done(ins, name)
 
     def keys(ps, name, out, k):
         V.wait_ge(sem[name], cnt[name])
         vw()
-        done(V.tensor_copy(T.ki[:, 0:k], ps[:, 0:k]))
+        done(V.tensor_copy(T.ki[:, 0:k], ps))
         vw()
         done(V.tensor_scalar(T.kj[:, 0:k], T.ki[:, 0:k], 65536 + NP - 1, None, A.bitwise_and))
         vw()
@@ -211,26 +245,18 @@ def rank_program(g, core, T, topo):
     def take(a, n, key, src, op):
         done(V.tensor_tensor(T.dd[:, D0 + a:D0 + a + n], T.pad[:].indirect(key), src, op))
 
-    def peek(a, n, key, bias):
-        done(S.activation(T.dd[:, D0 + a:D0 + a + n], T.pad[:].indirect(key), ActivationFunctionType.Identity,
-                          bias=bias), "sg")
+    def peek(out, table, key):
+        done(S.activation(out, table[:].indirect(key), F.Copy), "sg")
 
     def wrap(a, n):
         done(V.tensor_scalar(T.mm[:, a:a + n], T.dd[:, D0 + a:D0 + a + n], 0.0, -256.0, A.is_gt, A.mult))
 
-    def symbol0(ps, a, k0, k):
-        done(V.tensor_scalar(T.di[:, k0:k0 + k], ps[:, a:a + k], 256.0, None, A.add))
-
-    def route(h, n, parts):
-        k = n // 16
-        V.wait_ge(sem.pd, cnt["pd"])
-        for part in parts:
-            symbol0(T.pdst, *part)
-        vw()
-        done(V.tensor_scalar(T.dj[:, 0:k], T.di[:, 0:k], 4096 + NR - 1, None, A.bitwise_and))
-        vw()
+    def one_hot(to, k0, k):
         for d in range(NR):
-            done(V.tensor_scalar(T.oh[:, d:NR * k:NR], T.dj[:, 0:k], float(d), None, A.is_equal))
+            done(V.tensor_scalar(T.oh[:, NR * k0 + d:NR * (k0 + k):NR], to, float(d), None, A.is_equal))
+
+    def route(h, n, gap):
+        k = n // 16
         PE.wait_ge(sem.v, cnt["v"])
         PE.matmul(T.ppre[:, 0:NR * k], T.upp[:], T.oh[:, 0:NR * k], True, False)
         vw()
@@ -239,113 +265,158 @@ def rank_program(g, core, T, topo):
             done(V.tensor_tensor_scan(T.cum[:, d:NR * k:NR], o, o, float(block[d] * KC), A.add, A.max))
         PE.wait_ge(sem.v, cnt["v"])
         done(PE.matmul(T.ppre[:, 0:NR * k], T.ones[:], T.cum[:, 0:NR * k], False, True), "pp")
+        gap[0]()
+        taken = cnt["v"]
         V.wait_ge(sem.pp, cnt["pp"])
         done(V.tensor_tensor_scan(T.sel[:, 0:NR * k], T.rst[:, 0:NR * k], T.ppre[:, 0:NR * k], 1.0e6, A.min, A.max))
-        vw()
+        chosen = cnt["v"]
+        V.wait_ge(sem.v, taken)
+        gap[1]()
+        V.wait_ge(sem.v, chosen)
         done(V.tensor_scalar(T.off[:, 0:k], T.sel[:, NR - 1:NR * k:NR], BIG - (DUMP - 1), None, A.subtract))
-        vw()
+        placed = cnt["v"]
+        gap[2]()
+        V.wait_ge(sem.v, placed)
         done(V.tensor_tensor(wins[h][:, 0:WIN].indirect(T.off[:, 0:k]), T.dd[:, D0:D0 + n], T.mm[:, 0:n], A.add))
 
     def slots(h, q):
         return wins[h][:, DUMP + block[q] * CAP:DUMP + (block[q] + 1) * CAP]
 
+    def leg(to, eng, name, src, dst):
+        rid, pid = topo.addr(to, core)
+        cnt["snd"] += len(eng)
+        return RemoteDMATransfer(dst_ids=[DstId(rid=rid, pnc=pid)], dma_engine_mask=mask_of(eng), remote_sem=sem[name],
+                                 src=src, dst=dst)
+
     def send_keys(h):
         g.wait_ge(sem.v, cnt["v"])
-        legs = []
-        for i, q in enumerate(sorted(krelay)):
-            rid, pid = topo.addr(krelay[q], core)
-            eng = topo.engines(core, krelay[q])[i::len(krelay)]
-            legs.append(RemoteDMATransfer(dst_ids=[DstId(rid=rid, pnc=pid)], dma_engine_mask=mask_of(eng),
-                                          remote_sem=sem["rek%d" % h], src=kss[h][:, i * KC:(i + 1) * KC],
-                                          dst=kls[h][:, 0:KC]))
-            cnt["snd"] += len(eng)
+        legs = [leg(krelay[q], key_engines(T, topo, plan, rank, q), "rek%d" % h, kss[h][:, i * KC:(i + 1) * KC],
+                    kls[h][:, 0:KC]) for i, q in enumerate(sorted(krelay))]
         g.remote_dma_fused(legs, local_sem=sem.snd)
+        g.remote_dma_fused([cells_leg(h, turn[1])], local_sem=sem.snd)
+
+    def cells_leg(h, q):
+        to, name = (T.cores[q], "dir%d" % h) if q == direct else (relay[q], "rel%d" % h)
+        return leg(to, cell_engines(T, topo, plan, rank, q, h), name, slots(h, q), lands[h][:, 0:CAP])
 
     def send(h):
         g.wait_ge(sem.v, cnt["v"])
-        legs = []
-        for i, q in enumerate(sorted(relay)):
-            rid, pid = topo.addr(relay[q], core)
-            eng = topo.engines(core, relay[q])[i::len(relay)]
-            legs.append(RemoteDMATransfer(dst_ids=[DstId(rid=rid, pnc=pid)], dma_engine_mask=mask_of(eng),
-                                          remote_sem=sem["rel%d" % h], src=slots(h, q), dst=lands[h][:, 0:CAP]))
-            cnt["snd"] += len(eng)
-        g.remote_dma_fused(legs, local_sem=sem.snd)
-        rid, pid = topo.addr(T.cores[direct], core)
-        g.remote_dma(lands[h][:, 0:CAP], slots(h, direct), sem["dir%d" % h], sem.snd, pid, rid,
-                     topo.mask(core, T.cores[direct]))
-        cnt["snd"] += len(topo.engines(core, T.cores[direct]))
+        if h < HOPS - 1:
+            g.remote_dma_fused([cells_leg(h, turn[0]), cells_leg(h, direct)], local_sem=sem.snd)
+        else:
+            g.remote_dma_fused([cells_leg(h, q) for q in sorted(relay)], local_sem=sem.snd)
+            g.remote_dma_fused([cells_leg(h, direct)], local_sem=sem.snd)
 
     kh = HALF // 16
-    PE.wait_ge(sem.v, cnt["v"])
+    PE.wait_ge(sem.v, ready)
+    PE.wait_ge(sem.gi, made_p)
     PE.wait_ge(sem.ldc, 16)
-    pick(T.pdst[:, 0:2 * kh], T.selp, T.cel, HALF, 3 * HALF, "pd", True, False)
-    S.wait_ge(sem.v, cnt["v"])
+    pick(T.pdst[:, 0:2 * kh], selp, T.cel, HALF, 3 * HALF, "pd", True, False)
+    PE.wait_ge(sem.gi, made_d)
+    S.wait_ge(sem.v, ready)
     S.wait_ge(sem.ldp, 16)
-    peek(-HALF, HALF, T.key[:, kh:2 * kh], 0.0)
+    peek(T.dd[:, 0:HALF], T.pad, T.key[:, kh:2 * kh])
     V.wait_ge(sem.ldc, 16)
     vw()
     V.wait_ge(sem.ldp, 16)
     take(0, HALF, T.key[:, 0:kh], T.cel[:, 0:HALF], A.subtract)
     PE.wait_ge(sem.v, cnt["v"])
     PE.wait_ge(sem.sg, cnt["sg"])
-    pick(T.pdst[:, 0:2 * kh], T.seld, T.dd, 0, C0, "pd", False, True)
+    pick(T.pdst[:, 0:2 * kh], seld, T.dd, 0, C0, "pd", False, True)
+    PE.wait_ge(sem.gi, made_u)
+    done(S.activation(T.tab[:], T.pad[:], F.Copy), "sg")
+    half = cnt["v"]
     take(HALF, HALF, T.key[:, kh:2 * kh], T.cel[:, HALF:C0], A.subtract)
+    V.wait_ge(sem.v, half)
+    wrap(0, HALF)
+    V.wait_ge(sem.pd, cnt["pd"])
+    done(V.tensor_scalar(T.ki[:, kh:2 * kh], T.pdst[:, 0:kh], 256.0, None, A.add))
+    done(V.tensor_scalar(T.ki[:, 0:kh], T.pdst[:, kh:2 * kh], 256.0, None, A.add))
     vw()
-    wrap(0, C0)
-    route(0, C0, [(0, kh, kh), (kh, 0, kh)])
-    send(0)
+    done(V.tensor_scalar(T.kj[:, 0:2 * kh], T.ki[:, 0:2 * kh], NR - 1, None, A.bitwise_and))
+    vw()
+    one_hot(T.kj[:, 0:2 * kh], 0, 2 * kh)
 
-    near = direct ^ 1
-    far = [q for q in late if q != near][0]
-    pair = min(near, direct)
-    spare = -CAP if pair == 0 else HOLD
-    p0 = min(spare, pair * CAP)
-    parts = [((spare - p0) // 16, far * KC, KC), ((pair * CAP - p0) // 16, pair * KC, 2 * KC)]
+    def table0():
+        wrap(HALF, HALF)
+        V.wait_ge(sem.ldr, 16)
+        done(V.tensor_scalar(T.rwi[:], T.row[:], -1.0, float(256 + rank), A.mult, A.add))
+        V.wait_ge(sem.gi, made_r)
+
+    def table1():
+        done(V.tensor_scalar(T.rwj[:], T.rwi[:], NR - 1, None, A.bitwise_and))
+
+    def table2():
+        V.wait_ge(sem.v, cnt["v"] - 1)
+        done(V.tensor_copy(T.rwd[:], T.rwj[:]))
+        SY.wait_ge(sem.v, cnt["v"])
+        SY.wait_ge(sem.sg, cnt["sg"])
+        SY.dma_start(T.tab[0:128:16, 0:NP], T.rwd[:]).then_inc(sem.ldt, 16)
+
+    route(0, C0, [table0, table1, table2])
+    send(0)
+    PE.wait_ge(sem.gi, made_k)
+
+    at = {q: i for i, q in enumerate([q for q in range(NR) if q != rank] + [rank])}
+
+    def goal(q):
+        return T.dst[:, at[q] * CAP:(at[q] + 1) * CAP]
+
     for h in range(1, HOPS):
-        S.wait_ge(sem.v, cnt["v"])
-        w, land = wins[h - 1], lands[h - 1]
+        w, land, ks, kl = wins[h - 1], lands[h - 1], kss[h - 1], kls[h - 1]
         PE.wait_ge(sem.v, cnt["v"])
-        pick(T.pk0[:, 0:3 * KC], T.selk, w, DUMP, DUMP + 3 * CAP, "k0")
-        if h == 1:
-            vw()
-            done(V.memset(wins[2][:, DUMP:WIN], 0.0))
-        keys(T.pk0, "k0", kss[h - 1][:, 0:3 * KC], 3 * KC)
+        pick(T.pk0[:, 0:3 * KC], selk, w, DUMP, DUMP + 3 * CAP, "k0")
+        done(V.memset(wins[h][:, DUMP:WIN], EMPTY if h < HOPS - 1 else 0.0))
+        keys(T.pk0[:, 0:3 * KC], "k0", ks[:, 0:3 * KC], 3 * KC)
         send_keys(h - 1)
+        S.wait_ge(sem.v, cnt["v"])
+        if h == 1:
+            S.wait_ge(sem.ldt, 16)
+        peek(goal(rank), T.tab, ks[:, 2 * KC:3 * KC])
         vw()
-        take(rank * CAP, CAP, kss[h - 1][:, 2 * KC:3 * KC], slots(h - 1, rank), A.add)
-        own = cnt["v"]
+        take(rank * CAP, CAP, ks[:, 2 * KC:3 * KC], slots(h - 1, rank), A.add)
         vw()
         wrap(rank * CAP, CAP)
         PE.wait_ge(sem["dir%d" % (h - 1)], n_dir)
-        pick(T.pk1[:, 0:KC], T.selk, land, 0, CAP, "k1")
-        PE.wait_ge(sem.v, own)
-        pick(T.pk2[:, 0:KC], T.seld, T.dd, D0 + rank * CAP, D0 + (rank + 1) * CAP, "k2")
-        keys(T.pk1, "k1", T.key[:, 0:KC], KC)
+        pick(T.pk1[:, 0:4 * KC], selq, land, 0, CAP, "k1", m=4)
+        PE.wait_ge(sem.sg, cnt["sg"])
+        pick(T.pk2[:, 0:KC], selp, T.dst, 3 * CAP, 4 * CAP, "k2")
+        V.wait_ge(sem.k1, cnt["k1"])
+        done(V.tensor_tensor_scan(T.sel[:, 0:4 * KC], T.alt[:], T.pk1[:, 0:4 * KC], 0.0, A.add, A.max))
+        keys(T.sel[:, 3:4 * KC:4], "k1", T.key[:, 0:KC], KC)
+        S.wait_ge(sem.v, cnt["v"])
+        peek(goal(direct), T.tab, T.key[:, 0:KC])
         vw()
         take(direct * CAP, CAP, T.key[:, 0:KC], land[:, 0:CAP], A.add)
         vw()
         wrap(direct * CAP, CAP)
-        V.wait_ge(sem.k2, cnt["k2"])
-        symbol0(T.pk2, 0, rank * KC, KC)
         S.wait_ge(sem["lk%d" % (h - 1)], n_lk)
-        i = late.index(far)
-        peek(spare, CAP, kls[h - 1][:, i * KC:(i + 1) * KC], float(-rank))
-        V.wait_ge(sem["la%d" % (h - 1)], sum(n_late))
+        peek(goal(late[1]), T.tab, kl[:, KC:2 * KC])
+        if h == 1:
+            V.wait_ge(sem.ldt, 16)
         V.wait_ge(sem["lk%d" % (h - 1)], n_lk)
-        for q in (near, far):
+        done(V.tensor_copy(goal(late[0]), T.tab[:].indirect(kl[:, 0:KC])))
+        PE.wait_ge(sem.v, cnt["v"])
+        PE.wait_ge(sem.sg, cnt["sg"])
+        pick(T.pdst[:, 0:3 * KC], selp, T.dst, 0, 3 * CAP, "pd")
+
+        def handed(q):
             i = late.index(q)
-            take(q * CAP, CAP, kls[h - 1][:, i * KC:(i + 1) * KC], land[:, (1 + i) * CAP:(2 + i) * CAP], A.add)
-            if q == near:
-                first = cnt["v"]
-                PE.wait_ge(sem.v, first)
-                PE.wait_ge(sem.sg, cnt["sg"])
-                pick(T.pdst[:, 0:3 * KC], T.seld, T.dd, D0 + p0, D0 + p0 + 3 * CAP, "pd")
+            V.wait_ge(sem[("la%d", "lb%d")[i] % (h - 1)], n_late[i])
+            take(q * CAP, CAP, kl[:, i * KC:(i + 1) * KC], land[:, (1 + i) * CAP:(2 + i) * CAP], A.add)
+
+        handed(turn[0])
+        first = cnt["v"]
+        V.wait_ge(sem.k2, cnt["k2"])
+        one_hot(T.pk2[:, 0:KC], rank * KC, KC)
         V.wait_ge(sem.v, first)
-        wrap(near * CAP, CAP)
-        vw()
-        wrap(far * CAP, CAP)
-        route(h, HOLD, parts)
+        wrap(turn[0] * CAP, CAP)
+        V.wait_ge(sem.pd, cnt["pd"])
+        if rank > 0:
+            one_hot(T.pdst[:, 0:rank * KC], 0, rank * KC)
+        if rank < NR - 1:
+            one_hot(T.pdst[:, rank * KC:3 * KC], (rank + 1) * KC, (3 - rank) * KC)
+        route(h, HOLD, [lambda: handed(turn[1]), lambda: wrap(turn[1] * CAP, CAP), lambda: None])
         send(h)
 
     h = HOPS - 1
@@ -365,8 +436,7 @@ def rank_program(g, core, T, topo):
     out(late[0], land[:, CAP:2 * CAP])
     q = late[1]
     S.wait_ge(sem["lb%d" % h], n_late[1])
-    S.activation(T.yy[:, q * CAP:(q + 1) * CAP], land[:, 2 * CAP:3 * CAP], ActivationFunctionType.Copy,
-                 scale=-1.0).then_inc(sem.cs, 1)
+    S.activation(T.yy[:, q * CAP:(q + 1) * CAP], land[:, 2 * CAP:3 * CAP], F.Copy, scale=-1.0).then_inc(sem.cs, 1)
     S.wait_ge(sem.cs, 1)
     S.dma_start(T.y[:, q * CAP:(q + 1) * CAP], T.yy[:, q * CAP:(q + 1) * CAP]).then_inc(sem.st2, 16)
     S.wait_ge(sem.st2, 16)

from concourse.bass import DstId, RemoteDMATransfer
from concourse.mybir import AluOpType, ActivationFunctionType

NR, C0, CAP, NP, HOPS = 4, 896, 320, 4096, 3
HOLD = NR * CAP
KC = CAP // 16
DUMP = HOLD + 112
WIN = DUMP + HOLD
BIG = 3072.0
EMPTY = -256.0
NOPAD = 2304.0
HALF = C0 // 2
D0 = HALF
SEG = NP // 16
TAKE, KEEP = 1.0e6, 131072.0

SCRATCH = {
    "pad": ("sbuf", [128, NP + 16], "bfloat16"),
    "tab": ("sbuf", [128, NP + 16], "bfloat16"),
    "row": ("sbuf", [128, SEG], "bfloat16"),
    "rwi": ("sbuf", [128, SEG], "int32"),
    "rwj": ("sbuf", [128, SEG], "int32"),
    "rwd": ("sbuf", [128, SEG], "bfloat16"),
    "cel": ("sbuf", [128, C0 + HALF], "bfloat16"),
    "fst": ("sbuf", [128, C0 // 16], "int32"),
    "win0": ("sbuf", [128, WIN], "bfloat16"),
    "win1": ("sbuf", [128, WIN], "bfloat16"),
    "win2": ("sbuf", [128, WIN], "bfloat16"),
    "land0": ("sbuf", [128, 3 * CAP], "bfloat16"),
    "land1": ("sbuf", [128, 3 * CAP], "bfloat16"),
    "land2": ("sbuf", [128, 3 * CAP], "bfloat16"),
    "dd": ("sbuf", [128, D0 + HOLD], "bfloat16"),
    "dst": ("sbuf", [128, HOLD], "bfloat16"),
    "mm": ("sbuf", [128, HOLD], "bfloat16"),
    "yy": ("sbuf", [128, HOLD], "float32"),
    "pc": ("sbuf", [128, 8], "int32"),
    "col": ("sbuf", [128, 8], "float32"),
    "sels": ("sbuf", [128, 640], "bfloat16"),
    "ones": ("sbuf", [128, 128], "bfloat16"),
    "upp": ("sbuf", [128, 128], "bfloat16"),
    "rst": ("sbuf", [128, 4 * 80], "float32"),
    "ki": ("sbuf", [128, 80], "int32"),
    "kj": ("sbuf", [128, 80], "int32"),
    "key": ("sbuf", [128, 80], "uint16"),
    "ks0": ("sbuf", [128, 64], "uint16"),
    "ks1": ("sbuf", [128, 64], "uint16"),
    "kl0": ("sbuf", [128, 64], "uint16"),
    "kl1": ("sbuf", [128, 64], "uint16"),
    "oh": ("sbuf", [128, 4 * 80], "bfloat16"),
    "cum": ("sbuf", [128, 4 * 80], "bfloat16"),
    "sel": ("sbuf", [128, 4 * 80], "float32"),
    "off": ("sbuf", [128, 80], "uint16"),
    "pk0": ("psum", [128, 512], "float32"),
    "pk1": ("psum", [128, 512], "float32"),
    "pk2": ("psum", [128, 512], "float32"),
    "alt": ("sbuf", [128, 80], "float32"),
    "pdst": ("psum", [128, 512], "float32"),
    "ppre": ("psum", [128, 512], "float32"),
}
SEMAPHORES = (["ldp", "ldf", "ldc", "ldr", "ldt", "gi", "v", "k0", "k1", "k2", "pd", "pp", "snd", "fwd", "cs", "st", "st2", "sg"]
              + ["%s%d" % (n, h) for n in ("dir", "la", "lb", "rel") for h in range(HOPS)]
              + ["%s%d" % (n, h) for n in ("lk", "rek") for h in range(HOPS - 1)])


def routes(T, topo):
    plan = []
    for r, src in enumerate(T.cores):
        direct, relay, krelay = [], {}, {}
        for q, dst in enumerate(T.cores):
            if q == r:
                continue
            if topo.may_write(src, dst):
                direct.append(q)
                continue
            same_die = topo.host(src) == topo.host(dst)
            cand = [c for c in topo.cores_of(src)
                    if c not in T.cores and c not in relay.values() and topo.may_write(c, dst)]
            want = [c for c in cand if (topo.die(c) == topo.die(src)) == same_die]
            relay[q] = (want or cand)[0]
        for q in relay:
            cand = [c for c in topo.cores_of(src) if c not in T.cores and c not in relay.values()
                    and c not in krelay.values() and topo.may_write(c, T.cores[q])]
            want = [c for c in cand if topo.die(c) == topo.die(relay[q])]
            krelay[q] = (want or cand)[0]
        plan.append((direct, relay, krelay))
    return plan


def mask_of(engines):
    m = 0
    for e in engines:
        m |= 1 << e
    return m


def late_of(plan, q):
    return [r for r in range(NR) if q in plan[r][1]]


def key_engines(T, topo, plan, src, dst):
    krelay = plan[src][2]
    return topo.engines(T.cores[src], krelay[dst])[sorted(krelay).index(dst)::len(krelay)]


def cell_engines(T, topo, plan, src, dst, h):
    direct, relay, _ = plan[src]
    out = topo.engines(T.cores[src], T.cores[direct[0]])
    if dst not in relay:
        return out
    every = topo.engines(T.cores[src], relay[dst])
    if h == HOPS - 1:
        return every[sorted(relay).index(dst)::len(relay)]
    return [e for e in every if e not in out]


def relay_program(g, core, T, topo, plan, src, dst):
    lands = [T.land0, T.land1, T.land2]
    i = late_of(plan, dst).index(src)
    rid, pid = topo.addr(T.cores[dst], core)
    n_out = len(topo.engines(core, T.cores[dst]))
    for h in range(HOPS):
        g.wait_ge(T.sem["rel%d" % h], len(cell_engines(T, topo, plan, src, dst, h)))
        name = ("la%d", "lb%d")[i] % h
        g.remote_dma(lands[h][:, (1 + i) * CAP:(2 + i) * CAP], lands[h][:, 0:CAP], T.sem[name], T.sem.fwd, pid, rid,
                     topo.mask(core, T.cores[dst]))
    g.wait_ge(T.sem.fwd, HOPS * n_out)


def key_relay_program(g, core, T, topo, plan, src, dst):
    kls = [T.kl0, T.kl1]
    i = late_of(plan, dst).index(src)
    n_in = len(key_engines(T, topo, plan, src, dst))
    rid, pid = topo.addr(T.cores[dst], core)
    for h in range(HOPS - 1):
        g.wait_ge(T.sem["rek%d" % h], n_in)
        g.remote_dma(kls[h][:, i * KC:(i + 1) * KC], kls[h][:, 0:KC], T.sem["lk%d" % h], T.sem.fwd, pid, rid,
                     topo.mask(core, T.cores[dst]))
    g.wait_ge(T.sem.fwd, (HOPS - 1) * len(topo.engines(core, T.cores[dst])))


def rank_program(g, core, T, topo):
    plan = routes(T, topo)
    rank = T.rank_of(core)
    if rank is None:
        for r in range(NR):
            for q, c in plan[r][1].items():
                if c == core:
                    relay_program(g, core, T, topo, plan, r, q)
            for q, c in plan[r][2].items():
                if c == core:
                    key_relay_program(g, core, T, topo, plan, r, q)
        return

    A, F = AluOpType, ActivationFunctionType
    V, PE, S, SY = g.vector, g.tensor, g.scalar, g.sync
    sem = T.sem
    wins = [T.win0, T.win1, T.win2]
    lands = [T.land0, T.land1, T.land2]
    direct = plan[rank][0][0]
    relay = plan[rank][1]
    late = late_of(plan, rank)
    n_dir = len(topo.engines(T.cores[direct], core))
    n_late = [len(topo.engines(plan[r][1][rank], core)) for r in late]
    krelay = plan[rank][2]
    n_lk = sum(len(topo.engines(plan[r][2][rank], core)) for r in late)
    kss, kls = [T.ks0, T.ks1], [T.kl0, T.kl1]
    block = {q: i for i, q in enumerate(sorted(relay) + [rank, direct])}
    turn = sorted(late, key=lambda q: topo.host(T.cores[q]) != topo.host(core))
    cnt = {"v": 0, "k0": 0, "k1": 0, "k2": 0, "pd": 0, "pp": 0, "snd": 0, "st": 0, "sg": 0, "gi": 0}

    def done(ins, name="v", n=1):
        ins.then_inc(sem[name], n)
        cnt[name] += n

    def vw():
        V.wait_ge(sem.v, cnt["v"])

    S.dma_start(T.fst[:], T.first[:]).then_inc(sem.ldf, 16)
    SY.dma_start(T.cel[:, 0:C0], T.cells[:]).then_inc(sem.ldc, 16)
    SY.dma_start(T.pad[:, 0:NP], T.pads[:]).then_inc(sem.ldp, 16)
    SY.dma_start(T.row[:], T.pads[0:128:16, :]).then_inc(sem.ldr, 16)

    selp, seld, selk, selq = 0, 160, 320, 480
    done(V.memset(T.sels[:], 0.0))
    done(V.memset(T.upp[:], -1.0))
    done(V.memset(T.ones[:], 1.0))
    filled = cnt["v"]
    done(V.memset(T.cel[:, C0:C0 + HALF], 0.0))
    done(V.memset(T.pad[:, NP:NP + 16], NOPAD))
    done(V.memset(T.alt[:], -TAKE))
    done(V.memset(wins[0][:, DUMP:WIN], EMPTY))

    def mark(ap, pattern, op, fill, base, by):
        done(g.affine_select(ap, ap, pattern, op, fill, base, by), "gi")
        return cnt["gi"]

    def weight(ap, pattern, symbol, w):
        return mark(ap, pattern, A.not_equal, w, symbol - 1000 * (pattern[-1][1] - 1), -1)

    one, four = [[16, 9], [1000, 16]], [[16, 9], [0, 4], [1000, 4]]
    done(g.iota(T.pc[:, 0:1], [[1, 1]], 0, 1), "gi")
    g.wait_ge(sem.v, filled)
    made_p = weight(T.sels[:, 0:144], one, 0, 1.0)
    made_d = weight(T.sels[:, 160:304], one, 0, -1.0)
    mark(T.upp[:], [[-1, 128]], A.is_gt, 0.0, 0, 1)
    g.wait_ge(sem.gi, mark(T.ones[:], [[-16, 8], [0, 16]], A.is_ge, 0.0, 0, 1))
    mark(T.upp[:], [[16, 8], [0, 16]], A.is_ge, 0.0, 15, -1)
    g.wait_ge(sem.gi, mark(T.ones[:], [[16, 8], [0, 16]], A.is_ge, 0.0, 15, -1))
    made_u = mark(T.upp[:], [[-1, 128]], A.not_equal, BIG, 0, 1)
    done(g.iota(T.rst[:], [[-16, 80], [20000, 4]], int(BIG), -1, allow_small_or_imprecise_dtypes=True), "gi")
    made_r = cnt["gi"]
    weight(T.sels[:, 320:464], one, 1, -1.0)
    g.wait_ge(sem.gi, weight(T.sels[:, 492:636], four, 1, -1.0))
    weight(T.sels[:, 320:464], one, 2, -256.0)
    made_k = weight(T.sels[:, 492:636], four, 2, -256.0)

    V.wait_ge(sem.gi, 1)
    done(V.tensor_scalar(T.pc[:, 1:2], T.pc[:, 0:1], 15, None, A.bitwise_and))
    vw()
    for i in (1, 2, 3):
        done(V.tensor_scalar(T.col[:, i:i + 1], T.pc[:, 1:2], 4.0 * i, TAKE + KEEP, A.is_lt, A.mult))
    vw()
    for i in (1, 2, 3):
        done(V.tensor_scalar(T.alt[:, i:4 * KC:4], T.alt[:, i:4 * KC:4], T.col[:, i:i + 1], None, A.add))
    V.wait_ge(sem.ldf, 16)
    done(V.tensor_copy(T.key[:, 0:C0 // 16], T.fst[:]))
    ready = cnt["v"]

    def pick(out, sel, data, a, b, name, start=True, stop=True, m=16):
        for t in range(m):
            ins = PE.matmul(out, T.sels[:, sel + 15 - t:sel + 143 - t], data[:, a + t:b:m], start and t == 0,
                            stop and t == m - 1)
        if stop:
            done(ins, name)

    def keys(ps, name, out, k):
        V.wait_ge(sem[name], cnt[name])
        vw()
        done(V.tensor_copy(T.ki[:, 0:k], ps))
        vw()
        done(V.tensor_scalar(T.kj[:, 0:k], T.ki[:, 0:k], 65536 + NP - 1, None, A.bitwise_and))
        vw()
        done(V.tensor_scalar(out, T.kj[:, 0:k], float(NP), None, A.min))

    def take(a, n, key, src, op):
        done(V.tensor_tensor(T.dd[:, D0 + a:D0 + a + n], T.pad[:].indirect(key), src, op))

    def peek(out, table, key):
        done(S.activation(out, table[:].indirect(key), F.Copy), "sg")

    def wrap(a, n):
        done(V.tensor_scalar(T.mm[:, a:a + n], T.dd[:, D0 + a:D0 + a + n], 0.0, -256.0, A.is_gt, A.mult))

    def one_hot(to, k0, k):
        for d in range(NR):
            done(V.tensor_scalar(T.oh[:, NR * k0 + d:NR * (k0 + k):NR], to, float(d), None, A.is_equal))

    def route(h, n, gap):
        k = n // 16
        PE.wait_ge(sem.v, cnt["v"])
        PE.matmul(T.ppre[:, 0:NR * k], T.upp[:], T.oh[:, 0:NR * k], True, False)
        vw()
        for d in range(NR):
            o = T.oh[:, d:NR * k:NR]
            done(V.tensor_tensor_scan(T.cum[:, d:NR * k:NR], o, o, float(block[d] * KC), A.add, A.max))
        PE.wait_ge(sem.v, cnt["v"])
        done(PE.matmul(T.ppre[:, 0:NR * k], T.ones[:], T.cum[:, 0:NR * k], False, True), "pp")
        gap[0]()
        taken = cnt["v"]
        V.wait_ge(sem.pp, cnt["pp"])
        done(V.tensor_tensor_scan(T.sel[:, 0:NR * k], T.rst[:, 0:NR * k], T.ppre[:, 0:NR * k], 1.0e6, A.min, A.max))
        chosen = cnt["v"]
        V.wait_ge(sem.v, taken)
        gap[1]()
        V.wait_ge(sem.v, chosen)
        done(V.tensor_scalar(T.off[:, 0:k], T.sel[:, NR - 1:NR * k:NR], BIG - (DUMP - 1), None, A.subtract))
        placed = cnt["v"]
        gap[2]()
        V.wait_ge(sem.v, placed)
        done(V.tensor_tensor(wins[h][:, 0:WIN].indirect(T.off[:, 0:k]), T.dd[:, D0:D0 + n], T.mm[:, 0:n], A.add))

    def slots(h, q):
        return wins[h][:, DUMP + block[q] * CAP:DUMP + (block[q] + 1) * CAP]

    def leg(to, eng, name, src, dst):
        rid, pid = topo.addr(to, core)
        cnt["snd"] += len(eng)
        return RemoteDMATransfer(dst_ids=[DstId(rid=rid, pnc=pid)], dma_engine_mask=mask_of(eng), remote_sem=sem[name],
                                 src=src, dst=dst)

    def send_keys(h):
        g.wait_ge(sem.v, cnt["v"])
        legs = [leg(krelay[q], key_engines(T, topo, plan, rank, q), "rek%d" % h, kss[h][:, i * KC:(i + 1) * KC],
                    kls[h][:, 0:KC]) for i, q in enumerate(sorted(krelay))]
        g.remote_dma_fused(legs, local_sem=sem.snd)
        g.remote_dma_fused([cells_leg(h, turn[1])], local_sem=sem.snd)

    def cells_leg(h, q):
        to, name = (T.cores[q], "dir%d" % h) if q == direct else (relay[q], "rel%d" % h)
        return leg(to, cell_engines(T, topo, plan, rank, q, h), name, slots(h, q), lands[h][:, 0:CAP])

    def send(h):
        g.wait_ge(sem.v, cnt["v"])
        if h < HOPS - 1:
            g.remote_dma_fused([cells_leg(h, turn[0]), cells_leg(h, direct)], local_sem=sem.snd)
        else:
            g.remote_dma_fused([cells_leg(h, q) for q in sorted(relay)], local_sem=sem.snd)
            g.remote_dma_fused([cells_leg(h, direct)], local_sem=sem.snd)

    kh = HALF // 16
    PE.wait_ge(sem.v, ready)
    PE.wait_ge(sem.gi, made_p)
    PE.wait_ge(sem.ldc, 16)
    pick(T.pdst[:, 0:2 * kh], selp, T.cel, HALF, 3 * HALF, "pd", True, False)
    PE.wait_ge(sem.gi, made_d)
    S.wait_ge(sem.v, ready)
    S.wait_ge(sem.ldp, 16)
    peek(T.dd[:, 0:HALF], T.pad, T.key[:, kh:2 * kh])
    V.wait_ge(sem.ldc, 16)
    vw()
    V.wait_ge(sem.ldp, 16)
    take(0, HALF, T.key[:, 0:kh], T.cel[:, 0:HALF], A.subtract)
    PE.wait_ge(sem.v, cnt["v"])
    PE.wait_ge(sem.sg, cnt["sg"])
    pick(T.pdst[:, 0:2 * kh], seld, T.dd, 0, C0, "pd", False, True)
    PE.wait_ge(sem.gi, made_u)
    done(S.activation(T.tab[:], T.pad[:], F.Copy), "sg")
    half = cnt["v"]
    take(HALF, HALF, T.key[:, kh:2 * kh], T.cel[:, HALF:C0], A.subtract)
    V.wait_ge(sem.v, half)
    wrap(0, HALF)
    V.wait_ge(sem.pd, cnt["pd"])
    done(V.tensor_scalar(T.ki[:, kh:2 * kh], T.pdst[:, 0:kh], 256.0, None, A.add))
    done(V.tensor_scalar(T.ki[:, 0:kh], T.pdst[:, kh:2 * kh], 256.0, None, A.add))
    vw()
    done(V.tensor_scalar(T.kj[:, 0:2 * kh], T.ki[:, 0:2 * kh], NR - 1, None, A.bitwise_and))
    vw()
    one_hot(T.kj[:, 0:2 * kh], 0, 2 * kh)

    def table0():
        wrap(HALF, HALF)
        V.wait_ge(sem.ldr, 16)
        done(V.tensor_scalar(T.rwi[:], T.row[:], -1.0, float(256 + rank), A.mult, A.add))
        V.wait_ge(sem.gi, made_r)

    def table1():
        done(V.tensor_scalar(T.rwj[:], T.rwi[:], NR - 1, None, A.bitwise_and))

    def table2():
        V.wait_ge(sem.v, cnt["v"] - 1)
        done(V.tensor_copy(T.rwd[:], T.rwj[:]))
        SY.wait_ge(sem.v, cnt["v"])
        SY.wait_ge(sem.sg, cnt["sg"])
        SY.dma_start(T.tab[0:128:16, 0:NP], T.rwd[:]).then_inc(sem.ldt, 16)

    route(0, C0, [table0, table1, table2])
    send(0)
    PE.wait_ge(sem.gi, made_k)

    at = {q: i for i, q in enumerate([q for q in range(NR) if q != rank] + [rank])}

    def goal(q):
        return T.dst[:, at[q] * CAP:(at[q] + 1) * CAP]

    for h in range(1, HOPS):
        w, land, ks, kl = wins[h - 1], lands[h - 1], kss[h - 1], kls[h - 1]
        PE.wait_ge(sem.v, cnt["v"])
        pick(T.pk0[:, 0:3 * KC], selk, w, DUMP, DUMP + 3 * CAP, "k0")
        done(V.memset(wins[h][:, DUMP:WIN], EMPTY if h < HOPS - 1 else 0.0))
        keys(T.pk0[:, 0:3 * KC], "k0", ks[:, 0:3 * KC], 3 * KC)
        send_keys(h - 1)
        S.wait_ge(sem.v, cnt["v"])
        if h == 1:
            S.wait_ge(sem.ldt, 16)
        peek(goal(rank), T.tab, ks[:, 2 * KC:3 * KC])
        vw()
        take(rank * CAP, CAP, ks[:, 2 * KC:3 * KC], slots(h - 1, rank), A.add)
        vw()
        wrap(rank * CAP, CAP)
        PE.wait_ge(sem["dir%d" % (h - 1)], n_dir)
        pick(T.pk1[:, 0:4 * KC], selq, land, 0, CAP, "k1", m=4)
        PE.wait_ge(sem.sg, cnt["sg"])
        pick(T.pk2[:, 0:KC], selp, T.dst, 3 * CAP, 4 * CAP, "k2")
        V.wait_ge(sem.k1, cnt["k1"])
        done(V.tensor_tensor_scan(T.sel[:, 0:4 * KC], T.alt[:], T.pk1[:, 0:4 * KC], 0.0, A.add, A.max))
        keys(T.sel[:, 3:4 * KC:4], "k1", T.key[:, 0:KC], KC)
        S.wait_ge(sem.v, cnt["v"])
        peek(goal(direct), T.tab, T.key[:, 0:KC])
        vw()
        take(direct * CAP, CAP, T.key[:, 0:KC], land[:, 0:CAP], A.add)
        vw()
        wrap(direct * CAP, CAP)
        S.wait_ge(sem["lk%d" % (h - 1)], n_lk)
        peek(goal(late[1]), T.tab, kl[:, KC:2 * KC])
        if h == 1:
            V.wait_ge(sem.ldt, 16)
        V.wait_ge(sem["lk%d" % (h - 1)], n_lk)
        done(V.tensor_copy(goal(late[0]), T.tab[:].indirect(kl[:, 0:KC])))
        PE.wait_ge(sem.v, cnt["v"])
        PE.wait_ge(sem.sg, cnt["sg"])
        pick(T.pdst[:, 0:3 * KC], selp, T.dst, 0, 3 * CAP, "pd")

        def handed(q):
            i = late.index(q)
            V.wait_ge(sem[("la%d", "lb%d")[i] % (h - 1)], n_late[i])
            take(q * CAP, CAP, kl[:, i * KC:(i + 1) * KC], land[:, (1 + i) * CAP:(2 + i) * CAP], A.add)

        handed(turn[0])
        first = cnt["v"]
        V.wait_ge(sem.k2, cnt["k2"])
        one_hot(T.pk2[:, 0:KC], rank * KC, KC)
        V.wait_ge(sem.v, first)
        wrap(turn[0] * CAP, CAP)
        V.wait_ge(sem.pd, cnt["pd"])
        if rank > 0:
            one_hot(T.pdst[:, 0:rank * KC], 0, rank * KC)
        if rank < NR - 1:
            one_hot(T.pdst[:, rank * KC:3 * KC], (rank + 1) * KC, (3 - rank) * KC)
        route(h, HOLD, [lambda: handed(turn[1]), lambda: wrap(turn[1] * CAP, CAP), lambda: None])
        send(h)

    h = HOPS - 1
    land = lands[h]

    def out(q, src):
        vw()
        done(V.tensor_scalar(T.yy[:, q * CAP:(q + 1) * CAP], src, -1.0, None, A.mult))
        SY.wait_ge(sem.v, cnt["v"])
        done(SY.dma_start(T.y[:, q * CAP:(q + 1) * CAP], T.yy[:, q * CAP:(q + 1) * CAP]), "st", 16)

    SY.wait_ge(sem.snd, cnt["snd"])
    out(rank, slots(h, rank))
    V.wait_ge(sem["dir%d" % h], n_dir)
    out(direct, land[:, 0:CAP])
    V.wait_ge(sem["la%d" % h], n_late[0])
    out(late[0], land[:, CAP:2 * CAP])
    q = late[1]
    S.wait_ge(sem["lb%d" % h], n_late[1])
    S.activation(T.yy[:, q * CAP:(q + 1) * CAP], land[:, 2 * CAP:3 * CAP], F.Copy, scale=-1.0).then_inc(sem.cs, 1)
    S.wait_ge(sem.cs, 1)
    S.dma_start(T.y[:, q * CAP:(q + 1) * CAP], T.yy[:, q * CAP:(q + 1) * CAP]).then_inc(sem.st2, 16)
    S.wait_ge(sem.st2, 16)
    SY.wait_ge(sem.st, cnt["st"])
    g.wait_ge(sem.snd, cnt["snd"])
